import numpy as np
import ml_dtypes


def mxq(x, axis, fmt="e4m3"):
    dtype, down = {"e4m3": (ml_dtypes.float8_e4m3fn, 7), "e5m2": (ml_dtypes.float8_e5m2, 14)}[fmt]
    v = np.moveaxis(np.asarray(x, np.float32).astype(ml_dtypes.bfloat16).astype(np.float64), axis, -1)
    blocks = v.reshape(v.shape[:-1] + (-1, 32))
    amax = np.abs(blocks).max(-1, keepdims=True)
    byte = np.maximum(np.where(amax > 0, np.frexp(amax)[1] - 1 + 127, 0) - down, 1)
    scale = np.exp2(byte - 127.0)
    codes = (blocks / scale).astype(np.float32).astype(dtype).astype(np.float64)
    return np.moveaxis((codes * scale).reshape(v.shape), -1, axis)


WIDE = False


def mx_kscale(k):
    if not WIDE:
        return np.ones(k)
    levels = np.array([10, -10, 5, -5, 0])
    if k % 512:
        return np.exp2(np.random.permutation(np.resize(levels, k // 32))).repeat(32)
    a = np.empty((k // 512, 16))
    for p in range(k // 512):
        a[p, :8] = np.random.permutation(np.resize(levels, 8))
        for g in range(8):
            far = levels[np.abs(levels - a[p, g]) >= 10]
            a[p, g + 8] = far[np.random.randint(len(far))]
    return np.exp2(a.ravel()).repeat(32)


def f64(x):
    return np.asarray(x).astype(np.float64)


def striped8(idx):
    return np.asarray(idx).reshape(8, -1, 16).transpose(0, 2, 1).reshape(128, -1).astype(np.uint16)


def unstriped8(offs):
    return offs.reshape(8, 16, -1).transpose(0, 2, 1).reshape(8, -1).astype(np.int64)


def pick8(x, idx, run):
    r = np.arange(len(x))
    return x[r[:, None], idx[r % (8 * run) // run]]


E2M1 = np.array([0.0, 0.5, 1.0, 1.5, 2.0, 3.0, 4.0, 6.0, -0.0, -0.5, -1.0, -1.5, -2.0, -3.0, -4.0, -6.0])


def pack_weight(w, fmt):
    k, n = w.shape
    w = f64(np.asarray(w, np.float32).astype(ml_dtypes.bfloat16)).reshape(k // 32, 32, n)
    amax = np.abs(w).max(1)
    if fmt == "e4m3":
        byte = np.frexp(amax)[1] - 1 + 127 - 7
    else:
        mant, ex = np.frexp(amax / 6.0)
        byte = np.where(mant > 0.5, ex, ex - 1) + 127
    byte = np.clip(np.where(amax > 0, byte, 1), 1, 254)
    scaled = (w * np.exp2(127.0 - byte)[:, None, :]).reshape(k, n).astype(np.float32)
    by_word = np.ascontiguousarray(scaled.reshape(k // 512, 128, 4, n).transpose(0, 1, 3, 2))
    if fmt == "e4m3":
        words = by_word.astype(ml_dtypes.float8_e4m3fn).view(np.uint8)
    else:
        c = by_word.astype(ml_dtypes.float4_e2m1fn).view(np.uint8) & 0xF
        words = (c[..., 0::2] | (c[..., 1::2] << 4)).reshape(k // 512, 128, 2 * n)
    return np.ascontiguousarray(words), np.ascontiguousarray(byte.astype(np.uint8).reshape(k // 512, 16, n))


def unpack_weight(words, scales, fmt):
    g, _, n = scales.shape
    words = np.ascontiguousarray(words).reshape(g, 128, n, -1)
    if fmt == "e4m3":
        vals = words.view(ml_dtypes.float8_e4m3fn).astype(np.float64)
    else:
        nib = np.empty((g, 128, n, 4), np.uint8)
        nib[..., 0::2] = words & 0xF
        nib[..., 1::2] = words >> 4
        vals = E2M1[nib]
    vals = vals * np.repeat(np.exp2(scales.astype(np.float64) - 127.0), 8, axis=1)[..., None]
    return vals.transpose(0, 1, 3, 2).reshape(g * 512, n)


D, T, U, I, Q = 512, 1024, 1024, 512, 128


def setup_inputs():
    n = np.random.standard_normal
    idx = np.stack([np.random.permutation(T)[:I] for _ in range(8)])
    idx2 = np.stack([np.random.permutation(U)[:I] for _ in range(8)])
    idx3 = np.stack([np.random.permutation(T)[:I] for _ in range(8)])
    idx4 = np.stack([np.random.permutation(U)[:I] for _ in range(8)])
    fd = mx_kscale(D)
    keysp = pack_weight(n((D, T)) / fd[:, None], "e4m3")
    notesp = pack_weight(n((D, U)) / fd[:, None], "e2m1")
    return {
        "query": (n((D, Q)) * 1.0 / np.sqrt(D) * fd[:, None]).astype(np.float32),
        "keys_words": keysp[0],
        "keys_scales": keysp[1],
        "notes_words": notesp[0],
        "notes_scales": notesp[1],
        "offs": striped8(idx),
        "offs2": striped8(idx2),
        "offs3": striped8(idx3),
        "offs4": striped8(idx4),
    }


def reference(query, keys_words, keys_scales, notes_words, notes_scales, offs, offs2, offs3, offs4):
    idx = unstriped8(offs)
    idx2 = unstriped8(offs2)
    idx3 = unstriped8(offs3)
    idx4 = unstriped8(offs4)
    keysu = unpack_weight(keys_words, keys_scales, "e4m3")
    notesu = unpack_weight(notes_words, notes_scales, "e2m1")
    queryq = mxq(f64(query), 0, "e4m3")
    a = queryq.T @ keysu
    b = queryq.T @ notesu
    lo1 = np.minimum(pick8(a, idx, 16), pick8(b, idx2, 16))
    r = pick8(a, idx, 16) - lo1
    f1 = np.zeros((Q, T))
    f1[np.arange(Q)[:, None], idx[np.arange(Q) % 128 // 16]] = r
    f2 = np.zeros((Q, U))
    f2[np.arange(Q)[:, None], idx2[np.arange(Q) % 128 // 16]] = r
    aa = a - f1
    bb = b + f2
    y = np.minimum(pick8(aa, idx3, 16), pick8(bb, idx4, 16))
    return y

@@ -1,0 +1,153 @@
+from contextlib import ExitStack
+
+import concourse.mybir as mybir
+
+D, T, U, I, Q = 512, 1024, 1024, 512, 128
+FLOPS = 2 * D * Q * (T + U)
+
+F32 = mybir.dt.float32
+BF16 = mybir.dt.bfloat16
+I32 = mybir.dt.int32
+U32 = mybir.dt.uint32
+U16 = mybir.dt.uint16
+U8 = mybir.dt.uint8
+FP8X4 = mybir.dt.float8_e4m3fn_x4
+FP4X4 = mybir.dt.float4_e2m1fn_x4
+ALU = mybir.AluOpType
+COPY = mybir.ActivationFunctionType.Copy
+RELU = mybir.ActivationFunctionType.Relu
+
+P = 128
+PACK = 4
+HALF = I // 2
+LIST_COLS = I // 16
+HALF_COLS = HALF // 16
+
+
+def load_scale_plane(nc, plane, scales):
+    rows = scales[0].rearrange("(q r) n -> r q n", r=4)
+    words = plane[:].bitcast(I32)
+    for r in range(4):
+        nc.sync.dma_start(out=words[r:P:32, :], in_=rows[r].bitcast(I32))
+
+
+def tile_attend_sortedapart_two_kernel(
+    tc, query, keys_words, keys_scales, notes_words, notes_scales, offs, offs2, offs3, offs4, out
+):
+    nc = tc.nc
+    with ExitStack() as ctx:
+        sb = ctx.enter_context(tc.tile_pool(name="sb", bufs=1))
+        ps = ctx.enter_context(tc.psum_pool(name="ps", bufs=1))
+
+        notes_plane = sb.tile([P, U], U8, align_bytes=64)
+        keys_plane = sb.tile([P, T], U8, align_bytes=64)
+        f1 = sb.tile([P, T], F32)
+        f2 = sb.tile([P, U], F32)
+        nc.vector.memset(notes_plane[:].bitcast(U32), 0)
+        nc.vector.memset(keys_plane[:].bitcast(U32), 0)
+        nc.vector.memset(f1[:], 0.0)
+        nc.vector.memset(f2[:], 0.0)
+
+        q_raw = sb.tile([P, PACK, Q], F32)
+        nc.sync.dma_start(out=q_raw[:], in_=query.rearrange("(p t) q -> p t q", t=PACK))
+        notes = sb.tile([P, 2 * U], U8, align_bytes=64)
+        nc.sync.dma_start(out=notes[:].bitcast(I32), in_=notes_words[0].bitcast(I32))
+        load_scale_plane(nc, notes_plane, notes_scales)
+        keys = sb.tile([P, T], U32, align_bytes=64)
+        nc.sync.dma_start(
+            out=keys[:].bitcast(I32), in_=keys_words[0].rearrange("p n t -> p (n t)").bitcast(I32)
+        )
+        load_scale_plane(nc, keys_plane, keys_scales)
+        idx2 = sb.tile([P, LIST_COLS], U16)
+        nc.sync.dma_start(out=idx2[:], in_=offs2)
+        idx = sb.tile([P, LIST_COLS], U16)
+        nc.sync.dma_start(out=idx[:], in_=offs)
+        idx3 = sb.tile([P, LIST_COLS], U16)
+        nc.sync.dma_start(out=idx3[:], in_=offs3)
+        idx4 = sb.tile([P, LIST_COLS], U16)
+        nc.sync.dma_start(out=idx4[:], in_=offs4)
+
+        q_bf = sb.tile([P, Q, PACK], BF16, align_bytes=64)
+        nc.vector.tensor_copy(out=q_bf[:], in_=q_raw[:].rearrange("p t q -> p q t"))
+        q_codes = sb.tile([P, Q], U32, align_bytes=64)
+        q_plane = sb.tile([P, Q], U8, align_bytes=64)
+        nc.vector.quantize_mx(
+            out=q_codes[:].bitcast(FP8X4), scales=q_plane[:], in_=q_bf[:].rearrange("p q t -> p (q t)")
+        )
+
+        b = sb.tile([P, U], F32)
+        for j in range(2):
+            cols = slice(512 * j, 512 * (j + 1))
+            bank = ps.tile([P, 512], F32, name="b_bank%d" % j)
+            nc.tensor.matmul_mx(
+                out=bank[:],
+                lhsT=q_codes[:].bitcast(FP8X4),
+                lhsT_scale=q_plane[:],
+                rhs=notes[:, 1024 * j : 1024 * (j + 1)].bitcast(FP4X4),
+                rhs_scale=notes_plane[:, cols],
+                start=True,
+                stop=True,
+            )
+            if j == 0:
+                nc.scalar.activation(out=b[:, cols], in_=bank[:], func=COPY)
+            else:
+                nc.vector.tensor_copy(out=b[:, cols], in_=bank[:])
+
+        a = sb.tile([P, T], F32)
+        for j in range(4):
+            cols = slice(256 * j, 256 * (j + 1))
+            bank = ps.tile([P, 256], F32, name="a_bank%d" % j)
+            nc.tensor.matmul_mx(
+                out=bank[:],
+                lhsT=q_codes[:].bitcast(FP8X4),
+                lhsT_scale=q_plane[:],
+                rhs=keys[:, cols].bitcast(FP8X4),
+                rhs_scale=keys_plane[:, cols],
+                start=True,
+                stop=True,
+            )
+            if j == 0:
+                nc.scalar.activation(out=a[:, cols], in_=bank[:], func=COPY)
+            else:
+                nc.vector.tensor_copy(out=a[:, cols], in_=bank[:])
+
+        first, second = slice(0, HALF), slice(HALF, I)
+        first_cols, second_cols = slice(0, HALF_COLS), slice(HALF_COLS, LIST_COLS)
+
+        r = sb.tile([P, I], F32)
+        b_first = sb.tile([P, HALF], F32)
+        nc.scalar.activation(out=b_first[:], in_=b[:].indirect(idx2[:, first_cols]), func=COPY)
+        diff_first = sb.tile([P, HALF], F32)
+        nc.vector.tensor_tensor(
+            out=diff_first[:], in0=a[:].indirect(idx[:, first_cols]), in1=b_first[:], op=ALU.subtract
+        )
+        nc.vector.tensor_scalar_max(out=r[:, first], in0=diff_first[:], scalar1=0.0)
+        nc.vector.tensor_copy(out=f1[:].indirect(idx[:, first_cols]), in_=r[:, first])
+
+        b_second = sb.tile([P, HALF], F32)
+        nc.scalar.activation(out=b_second[:], in_=b[:].indirect(idx2[:, second_cols]), func=COPY)
+        a_second = sb.tile([P, HALF], F32)
+        nc.scalar.activation(out=a_second[:], in_=a[:].indirect(idx[:, second_cols]), func=COPY)
+        diff_second = sb.tile([P, HALF], F32)
+        nc.gpsimd.tensor_tensor(out=diff_second[:], in0=a_second[:], in1=b_second[:], op=ALU.subtract)
+        nc.scalar.activation(out=r[:, second], in_=diff_second[:], func=RELU)
+        nc.vector.tensor_copy(out=f1[:].indirect(idx[:, second_cols]), in_=r[:, second])
+
+        nc.vector.tensor_copy(out=f2[:].indirect(idx2[:]), in_=r[:])
+
+        aa = sb.tile([P, T], F32)
+        nc.gpsimd.tensor_tensor(out=aa[:], in0=a[:], in1=f1[:], op=ALU.subtract)
+        aa_listed = sb.tile([P, I], F32)
+        nc.scalar.activation(out=aa_listed[:], in_=aa[:].indirect(idx3[:]), func=COPY)
+
+        bb = sb.tile([P, U], F32)
+        nc.vector.tensor_tensor(out=bb[:], in0=b[:], in1=f2[:], op=ALU.add)
+        bb_first = sb.tile([P, HALF], F32)
+        nc.vector.tensor_copy(out=bb_first[:], in_=bb[:].indirect(idx4[:, first_cols]))
+        bb_second = sb.tile([P, HALF], F32)
+        nc.scalar.activation(out=bb_second[:], in_=bb[:].indirect(idx4[:, second_cols]), func=COPY)
+
+        for part, listed in ((first, bb_first), (second, bb_second)):
+            y = sb.tile([P, HALF], F32, name="y%d" % part.start)
+            nc.vector.tensor_tensor(out=y[:], in0=aa_listed[:, part], in1=listed[:], op=ALU.min)
+            nc.sync.dma_start(out=out[:, part], in_=y[:])

@@ -24,11 +24,11 @@ LIST_COLS = I // 16
 HALF_COLS = HALF // 16
 
 
-def load_scale_plane(nc, plane, scales):
+def load_scale_plane(queues, plane, scales):
     rows = scales[0].rearrange("(q r) n -> r q n", r=4)
     words = plane[:].bitcast(I32)
     for r in range(4):
-        nc.sync.dma_start(out=words[r:P:32, :], in_=rows[r].bitcast(I32))
+        queues[r].dma_start(out=words[r:P:32, :], in_=rows[r].bitcast(I32))
 
 
 def tile_attend_sortedapart_two_kernel(
@@ -41,23 +41,19 @@ def tile_attend_sortedapart_two_kernel(
 
         notes_plane = sb.tile([P, U], U8, align_bytes=64)
         keys_plane = sb.tile([P, T], U8, align_bytes=64)
-        f1 = sb.tile([P, T], F32)
-        f2 = sb.tile([P, U], F32)
         nc.vector.memset(notes_plane[:].bitcast(U32), 0)
         nc.vector.memset(keys_plane[:].bitcast(U32), 0)
-        nc.vector.memset(f1[:], 0.0)
-        nc.vector.memset(f2[:], 0.0)
 
-        q_raw = sb.tile([P, PACK, Q], F32)
+        q_raw = sb.tile([P, PACK, Q], F32, tag="raw_then_f2", align_bytes=64)
         nc.sync.dma_start(out=q_raw[:], in_=query.rearrange("(p t) q -> p t q", t=PACK))
         notes = sb.tile([P, 2 * U], U8, align_bytes=64)
         nc.sync.dma_start(out=notes[:].bitcast(I32), in_=notes_words[0].bitcast(I32))
-        load_scale_plane(nc, notes_plane, notes_scales)
+        load_scale_plane([nc.sync] * 4, notes_plane, notes_scales)
         keys = sb.tile([P, T], U32, align_bytes=64)
         nc.sync.dma_start(
             out=keys[:].bitcast(I32), in_=keys_words[0].rearrange("p n t -> p (n t)").bitcast(I32)
         )
-        load_scale_plane(nc, keys_plane, keys_scales)
+        load_scale_plane([nc.sync, nc.sync, nc.gpsimd, nc.gpsimd], keys_plane, keys_scales)
         idx2 = sb.tile([P, LIST_COLS], U16)
         nc.sync.dma_start(out=idx2[:], in_=offs2)
         idx = sb.tile([P, LIST_COLS], U16)
@@ -67,7 +63,7 @@ def tile_attend_sortedapart_two_kernel(
         idx4 = sb.tile([P, LIST_COLS], U16)
         nc.sync.dma_start(out=idx4[:], in_=offs4)
 
-        q_bf = sb.tile([P, Q, PACK], BF16, align_bytes=64)
+        q_bf = sb.tile([P, Q, PACK], BF16, tag="bf_then_f1", align_bytes=64)
         nc.vector.tensor_copy(out=q_bf[:], in_=q_raw[:].rearrange("p t q -> p q t"))
         q_codes = sb.tile([P, Q], U32, align_bytes=64)
         q_plane = sb.tile([P, Q], U8, align_bytes=64)
@@ -75,41 +71,45 @@ def tile_attend_sortedapart_two_kernel(
             out=q_codes[:].bitcast(FP8X4), scales=q_plane[:], in_=q_bf[:].rearrange("p q t -> p (q t)")
         )
 
-        b = sb.tile([P, U], F32)
-        for j in range(2):
-            cols = slice(512 * j, 512 * (j + 1))
-            bank = ps.tile([P, 512], F32, name="b_bank%d" % j)
-            nc.tensor.matmul_mx(
-                out=bank[:],
-                lhsT=q_codes[:].bitcast(FP8X4),
-                lhsT_scale=q_plane[:],
-                rhs=notes[:, 1024 * j : 1024 * (j + 1)].bitcast(FP4X4),
-                rhs_scale=notes_plane[:, cols],
-                start=True,
-                stop=True,
-            )
-            if j == 0:
-                nc.scalar.activation(out=b[:, cols], in_=bank[:], func=COPY)
-            else:
-                nc.vector.tensor_copy(out=b[:, cols], in_=bank[:])
+        f1 = sb.tile([P, T], F32, tag="bf_then_f1", align_bytes=64)
+        f2 = sb.tile([P, U], F32, tag="raw_then_f2", align_bytes=64)
+        nc.vector.memset(f1[:].bitcast(U32), 0)
+        nc.vector.memset(f2[:].bitcast(U32), 0)
 
+        b = sb.tile([P, U], F32)
+        b_bank0 = ps.tile([P, 512], F32)
+        nc.tensor.matmul_mx(out=b_bank0[:], lhsT=q_codes[:].bitcast(FP8X4), lhsT_scale=q_plane[:],
+                            rhs=notes[:, 0:1024].bitcast(FP4X4), rhs_scale=notes_plane[:, 0:512], start=True, stop=True)
+        nc.scalar.activation(out=b[:, 0:512], in_=b_bank0[:], func=COPY)
+        b_bank1 = ps.tile([P, 256], F32)
+        nc.tensor.matmul_mx(out=b_bank1[:], lhsT=q_codes[:].bitcast(FP8X4), lhsT_scale=q_plane[:],
+                            rhs=notes[:, 1024:1536].bitcast(FP4X4), rhs_scale=notes_plane[:, 512:768], start=True, stop=True)
+        nc.vector.tensor_copy(out=b[:, 512:768], in_=b_bank1[:])
+        b_bank2 = ps.tile([P, 256], F32)
+        nc.tensor.matmul_mx(out=b_bank2[:], lhsT=q_codes[:].bitcast(FP8X4), lhsT_scale=q_plane[:],
+                            rhs=notes[:, 1536:2048].bitcast(FP4X4), rhs_scale=notes_plane[:, 768:1024], start=True, stop=True)
+        nc.scalar.activation(out=b[:, 768:1024], in_=b_bank2[:], func=COPY)
         a = sb.tile([P, T], F32)
-        for j in range(4):
-            cols = slice(256 * j, 256 * (j + 1))
-            bank = ps.tile([P, 256], F32, name="a_bank%d" % j)
-            nc.tensor.matmul_mx(
-                out=bank[:],
-                lhsT=q_codes[:].bitcast(FP8X4),
-                lhsT_scale=q_plane[:],
-                rhs=keys[:, cols].bitcast(FP8X4),
-                rhs_scale=keys_plane[:, cols],
-                start=True,
-                stop=True,
-            )
-            if j == 0:
-                nc.scalar.activation(out=a[:, cols], in_=bank[:], func=COPY)
-            else:
-                nc.vector.tensor_copy(out=a[:, cols], in_=bank[:])
+        a_bank0 = ps.tile([P, 256], F32)
+        nc.tensor.matmul_mx(out=a_bank0[:], lhsT=q_codes[:].bitcast(FP8X4), lhsT_scale=q_plane[:],
+                            rhs=keys[:, 0:256].bitcast(FP8X4), rhs_scale=keys_plane[:, 0:256], start=True, stop=True)
+        nc.vector.tensor_copy(out=a[:, 0:256], in_=a_bank0[:])
+        a_bank1 = ps.tile([P, 256], F32)
+        nc.tensor.matmul_mx(out=a_bank1[:], lhsT=q_codes[:].bitcast(FP8X4), lhsT_scale=q_plane[:],
+                            rhs=keys[:, 256:512].bitcast(FP8X4), rhs_scale=keys_plane[:, 256:512], start=True, stop=True)
+        nc.vector.tensor_copy(out=a[:, 256:512], in_=a_bank1[:])
+        a_bank2 = ps.tile([P, 256], F32)
+        nc.tensor.matmul_mx(out=a_bank2[:], lhsT=q_codes[:].bitcast(FP8X4), lhsT_scale=q_plane[:],
+                            rhs=keys[:, 512:768].bitcast(FP8X4), rhs_scale=keys_plane[:, 512:768], start=True, stop=True)
+        nc.vector.tensor_copy(out=a[:, 512:768], in_=a_bank2[:])
+        a_bank3 = ps.tile([P, 128], F32)
+        nc.tensor.matmul_mx(out=a_bank3[:], lhsT=q_codes[:].bitcast(FP8X4), lhsT_scale=q_plane[:],
+                            rhs=keys[:, 768:896].bitcast(FP8X4), rhs_scale=keys_plane[:, 768:896], start=True, stop=True)
+        nc.vector.tensor_copy(out=a[:, 768:896], in_=a_bank3[:])
+        a_bank4 = ps.tile([P, 128], F32)
+        nc.tensor.matmul_mx(out=a_bank4[:], lhsT=q_codes[:].bitcast(FP8X4), lhsT_scale=q_plane[:],
+                            rhs=keys[:, 896:1024].bitcast(FP8X4), rhs_scale=keys_plane[:, 896:1024], start=True, stop=True)
+        nc.vector.tensor_copy(out=a[:, 896:1024], in_=a_bank4[:])
 
         first, second = slice(0, HALF), slice(HALF, I)
         first_cols, second_cols = slice(0, HALF_COLS), slice(HALF_COLS, LIST_COLS)
@@ -137,17 +137,25 @@ def tile_attend_sortedapart_two_kernel(
 
         aa = sb.tile([P, T], F32)
         nc.gpsimd.tensor_tensor(out=aa[:], in0=a[:], in1=f1[:], op=ALU.subtract)
-        aa_listed = sb.tile([P, I], F32)
-        nc.scalar.activation(out=aa_listed[:], in_=aa[:].indirect(idx3[:]), func=COPY)
+        aa_first = sb.tile([P, HALF], F32)
+        nc.scalar.activation(out=aa_first[:], in_=aa[:].indirect(idx3[:, first_cols]), func=COPY)
+        aa_second = sb.tile([P, HALF], F32)
+        nc.scalar.activation(out=aa_second[:], in_=aa[:].indirect(idx3[:, second_cols]), func=COPY)
 
         bb = sb.tile([P, U], F32)
-        nc.vector.tensor_tensor(out=bb[:], in0=b[:], in1=f2[:], op=ALU.add)
+        nc.vector.tensor_tensor(out=bb[:, 0:512], in0=b_bank0[:, 0:512], in1=f2[:, 0:512], op=ALU.add)
+        nc.vector.tensor_tensor(out=bb[:, 512:704], in0=b_bank1[:, 0:192], in1=f2[:, 512:704], op=ALU.add)
+        nc.gpsimd.tensor_tensor(out=bb[:, 704:1024], in0=b[:, 704:1024], in1=f2[:, 704:1024], op=ALU.add)
         bb_first = sb.tile([P, HALF], F32)
         nc.vector.tensor_copy(out=bb_first[:], in_=bb[:].indirect(idx4[:, first_cols]))
         bb_second = sb.tile([P, HALF], F32)
         nc.scalar.activation(out=bb_second[:], in_=bb[:].indirect(idx4[:, second_cols]), func=COPY)
-
-        for part, listed in ((first, bb_first), (second, bb_second)):
-            y = sb.tile([P, HALF], F32, name="y%d" % part.start)
-            nc.vector.tensor_tensor(out=y[:], in0=aa_listed[:, part], in1=listed[:], op=ALU.min)
-            nc.sync.dma_start(out=out[:, part], in_=y[:])
+        y0 = sb.tile([P, 256], F32)
+        nc.vector.tensor_tensor(out=y0[:], in0=aa_first[:, 0:256], in1=bb_first[:, 0:256], op=ALU.min)
+        nc.sync.dma_start(out=out[:, 0:256], in_=y0[:])
+        y1 = sb.tile([P, 128], F32)
+        nc.vector.tensor_tensor(out=y1[:], in0=aa_second[:, 0:128], in1=bb_second[:, 0:128], op=ALU.min)
+        nc.sync.dma_start(out=out[:, 256:384], in_=y1[:])
+        y2 = sb.tile([P, 128], F32)
+        nc.vector.tensor_tensor(out=y2[:], in0=aa_second[:, 128:256], in1=bb_second[:, 128:256], op=ALU.min)
+        nc.scalar.dma_start(out=out[:, 384:512], in_=y2[:])

@@ -44,7 +44,7 @@ def tile_attend_sortedapart_two_kernel(
         nc.vector.memset(notes_plane[:].bitcast(U32), 0)
         nc.vector.memset(keys_plane[:].bitcast(U32), 0)
 
-        q_raw = sb.tile([P, PACK, Q], F32, tag="raw_then_f2", align_bytes=64)
+        q_raw = sb.tile([P, PACK, Q], F32)
         nc.sync.dma_start(out=q_raw[:], in_=query.rearrange("(p t) q -> p t q", t=PACK))
         notes = sb.tile([P, 2 * U], U8, align_bytes=64)
         nc.sync.dma_start(out=notes[:].bitcast(I32), in_=notes_words[0].bitcast(I32))
@@ -72,9 +72,7 @@ def tile_attend_sortedapart_two_kernel(
         )
 
         f1 = sb.tile([P, T], F32, tag="bf_then_f1", align_bytes=64)
-        f2 = sb.tile([P, U], F32, tag="raw_then_f2", align_bytes=64)
         nc.vector.memset(f1[:].bitcast(U32), 0)
-        nc.vector.memset(f2[:].bitcast(U32), 0)
 
         b = sb.tile([P, U], F32)
         b_bank0 = ps.tile([P, 512], F32)
@@ -117,7 +115,7 @@ def tile_attend_sortedapart_two_kernel(
         r = sb.tile([P, I], F32)
         b_first = sb.tile([P, HALF], F32)
         nc.scalar.activation(out=b_first[:], in_=b[:].indirect(idx2[:, first_cols]), func=COPY)
-        diff_first = sb.tile([P, HALF], F32)
+        diff_first = sb.tile([P, HALF], F32, tag="diff")
         nc.vector.tensor_tensor(
             out=diff_first[:], in0=a[:].indirect(idx[:, first_cols]), in1=b_first[:], op=ALU.subtract
         )
@@ -126,11 +124,13 @@ def tile_attend_sortedapart_two_kernel(
 
         b_second = sb.tile([P, HALF], F32)
         nc.scalar.activation(out=b_second[:], in_=b[:].indirect(idx2[:, second_cols]), func=COPY)
-        a_second = sb.tile([P, HALF], F32)
+        a_second = sb.tile([P, HALF], F32, tag="a_second_then_f2")
         nc.scalar.activation(out=a_second[:], in_=a[:].indirect(idx[:, second_cols]), func=COPY)
-        diff_second = sb.tile([P, HALF], F32)
+        diff_second = sb.tile([P, HALF], F32, tag="diff")
         nc.gpsimd.tensor_tensor(out=diff_second[:], in0=a_second[:], in1=b_second[:], op=ALU.subtract)
         nc.scalar.activation(out=r[:, second], in_=diff_second[:], func=RELU)
+        f2 = sb.tile([P, U], F32, tag="a_second_then_f2")
+        nc.gpsimd.memset(f2[:], 0.0)
         nc.vector.tensor_copy(out=f1[:].indirect(idx[:, second_cols]), in_=r[:, second])
 
         nc.vector.tensor_copy(out=f2[:].indirect(idx2[:]), in_=r[:])
@@ -143,9 +143,7 @@ def tile_attend_sortedapart_two_kernel(
         nc.scalar.activation(out=aa_second[:], in_=aa[:].indirect(idx3[:, second_cols]), func=COPY)
 
         bb = sb.tile([P, U], F32)
-        nc.vector.tensor_tensor(out=bb[:, 0:512], in0=b_bank0[:, 0:512], in1=f2[:, 0:512], op=ALU.add)
-        nc.vector.tensor_tensor(out=bb[:, 512:704], in0=b_bank1[:, 0:192], in1=f2[:, 512:704], op=ALU.add)
-        nc.gpsimd.tensor_tensor(out=bb[:, 704:1024], in0=b[:, 704:1024], in1=f2[:, 704:1024], op=ALU.add)
+        nc.vector.tensor_tensor(out=bb[:], in0=b[:], in1=f2[:], op=ALU.add)
         bb_first = sb.tile([P, HALF], F32)
         nc.vector.tensor_copy(out=bb_first[:], in_=bb[:].indirect(idx4[:, first_cols]))
         bb_second = sb.tile([P, HALF], F32)
@@ -153,9 +151,6 @@ def tile_attend_sortedapart_two_kernel(
         y0 = sb.tile([P, 256], F32)
         nc.vector.tensor_tensor(out=y0[:], in0=aa_first[:, 0:256], in1=bb_first[:, 0:256], op=ALU.min)
         nc.sync.dma_start(out=out[:, 0:256], in_=y0[:])
-        y1 = sb.tile([P, 128], F32)
-        nc.vector.tensor_tensor(out=y1[:], in0=aa_second[:, 0:128], in1=bb_second[:, 0:128], op=ALU.min)
-        nc.sync.dma_start(out=out[:, 256:384], in_=y1[:])
-        y2 = sb.tile([P, 128], F32)
-        nc.vector.tensor_tensor(out=y2[:], in0=aa_second[:, 128:256], in1=bb_second[:, 128:256], op=ALU.min)
-        nc.scalar.dma_start(out=out[:, 384:512], in_=y2[:])
+        y1 = sb.tile([P, 256], F32)
+        nc.vector.tensor_tensor(out=y1[:], in0=aa_second[:, 0:256], in1=bb_second[:, 0:256], op=ALU.min)
+        nc.sync.dma_start(out=out[:, 256:512], in_=y1[:])

from contextlib import ExitStack

import concourse.mybir as mybir

D, T, U, I, Q = 512, 1024, 1024, 512, 128
FLOPS = 2 * D * Q * (T + U)

F32 = mybir.dt.float32
BF16 = mybir.dt.bfloat16
I32 = mybir.dt.int32
U32 = mybir.dt.uint32
U16 = mybir.dt.uint16
U8 = mybir.dt.uint8
FP8X4 = mybir.dt.float8_e4m3fn_x4
FP4X4 = mybir.dt.float4_e2m1fn_x4
ALU = mybir.AluOpType
COPY = mybir.ActivationFunctionType.Copy
RELU = mybir.ActivationFunctionType.Relu

P = 128
PACK = 4
HALF = I // 2
LIST_COLS = I // 16
HALF_COLS = HALF // 16


def load_scale_plane(queues, plane, scales):
    rows = scales[0].rearrange("(q r) n -> r q n", r=4)
    words = plane[:].bitcast(I32)
    for r in range(4):
        queues[r].dma_start(out=words[r:P:32, :], in_=rows[r].bitcast(I32))


def tile_attend_sortedapart_two_kernel(
    tc, query, keys_words, keys_scales, notes_words, notes_scales, offs, offs2, offs3, offs4, out
):
    nc = tc.nc
    with ExitStack() as ctx:
        sb = ctx.enter_context(tc.tile_pool(name="sb", bufs=1))
        ps = ctx.enter_context(tc.psum_pool(name="ps", bufs=1))

        notes_plane = sb.tile([P, U], U8, align_bytes=64)
        keys_plane = sb.tile([P, T], U8, align_bytes=64)
        nc.vector.memset(notes_plane[:].bitcast(U32), 0)
        nc.vector.memset(keys_plane[:].bitcast(U32), 0)

        q_raw = sb.tile([P, PACK, Q], F32)
        nc.sync.dma_start(out=q_raw[:], in_=query.rearrange("(p t) q -> p t q", t=PACK))
        notes = sb.tile([P, 2 * U], U8, align_bytes=64)
        nc.sync.dma_start(out=notes[:].bitcast(I32), in_=notes_words[0].bitcast(I32))
        load_scale_plane([nc.sync] * 4, notes_plane, notes_scales)
        keys = sb.tile([P, T], U32, align_bytes=64)
        nc.sync.dma_start(
            out=keys[:].bitcast(I32), in_=keys_words[0].rearrange("p n t -> p (n t)").bitcast(I32)
        )
        load_scale_plane([nc.sync, nc.sync, nc.gpsimd, nc.gpsimd], keys_plane, keys_scales)
        idx2 = sb.tile([P, LIST_COLS], U16)
        nc.sync.dma_start(out=idx2[:], in_=offs2)
        idx = sb.tile([P, LIST_COLS], U16)
        nc.sync.dma_start(out=idx[:], in_=offs)
        idx3 = sb.tile([P, LIST_COLS], U16)
        nc.sync.dma_start(out=idx3[:], in_=offs3)
        idx4 = sb.tile([P, LIST_COLS], U16)
        nc.sync.dma_start(out=idx4[:], in_=offs4)

        q_bf = sb.tile([P, Q, PACK], BF16, tag="bf_then_f1", align_bytes=64)
        nc.vector.tensor_copy(out=q_bf[:], in_=q_raw[:].rearrange("p t q -> p q t"))
        q_codes = sb.tile([P, Q], U32, align_bytes=64)
        q_plane = sb.tile([P, Q], U8, align_bytes=64)
        nc.vector.quantize_mx(
            out=q_codes[:].bitcast(FP8X4), scales=q_plane[:], in_=q_bf[:].rearrange("p q t -> p (q t)")
        )

        f1 = sb.tile([P, T], F32, tag="bf_then_f1", align_bytes=64)
        nc.vector.memset(f1[:].bitcast(U32), 0)

        b = sb.tile([P, U], F32)
        b_bank0 = ps.tile([P, 512], F32)
        nc.tensor.matmul_mx(out=b_bank0[:], lhsT=q_codes[:].bitcast(FP8X4), lhsT_scale=q_plane[:],
                            rhs=notes[:, 0:1024].bitcast(FP4X4), rhs_scale=notes_plane[:, 0:512], start=True, stop=True)
        nc.scalar.activation(out=b[:, 0:512], in_=b_bank0[:], func=COPY)
        b_bank1 = ps.tile([P, 256], F32)
        nc.tensor.matmul_mx(out=b_bank1[:], lhsT=q_codes[:].bitcast(FP8X4), lhsT_scale=q_plane[:],
                            rhs=notes[:, 1024:1536].bitcast(FP4X4), rhs_scale=notes_plane[:, 512:768], start=True, stop=True)
        nc.vector.tensor_copy(out=b[:, 512:768], in_=b_bank1[:])
        b_bank2 = ps.tile([P, 256], F32)
        nc.tensor.matmul_mx(out=b_bank2[:], lhsT=q_codes[:].bitcast(FP8X4), lhsT_scale=q_plane[:],
                            rhs=notes[:, 1536:2048].bitcast(FP4X4), rhs_scale=notes_plane[:, 768:1024], start=True, stop=True)
        nc.scalar.activation(out=b[:, 768:1024], in_=b_bank2[:], func=COPY)
        a = sb.tile([P, T], F32)
        a_bank0 = ps.tile([P, 256], F32)
        nc.tensor.matmul_mx(out=a_bank0[:], lhsT=q_codes[:].bitcast(FP8X4), lhsT_scale=q_plane[:],
                            rhs=keys[:, 0:256].bitcast(FP8X4), rhs_scale=keys_plane[:, 0:256], start=True, stop=True)
        nc.vector.tensor_copy(out=a[:, 0:256], in_=a_bank0[:])
        a_bank1 = ps.tile([P, 256], F32)
        nc.tensor.matmul_mx(out=a_bank1[:], lhsT=q_codes[:].bitcast(FP8X4), lhsT_scale=q_plane[:],
                            rhs=keys[:, 256:512].bitcast(FP8X4), rhs_scale=keys_plane[:, 256:512], start=True, stop=True)
        nc.vector.tensor_copy(out=a[:, 256:512], in_=a_bank1[:])
        a_bank2 = ps.tile([P, 256], F32)
        nc.tensor.matmul_mx(out=a_bank2[:], lhsT=q_codes[:].bitcast(FP8X4), lhsT_scale=q_plane[:],
                            rhs=keys[:, 512:768].bitcast(FP8X4), rhs_scale=keys_plane[:, 512:768], start=True, stop=True)
        nc.vector.tensor_copy(out=a[:, 512:768], in_=a_bank2[:])
        a_bank3 = ps.tile([P, 128], F32)
        nc.tensor.matmul_mx(out=a_bank3[:], lhsT=q_codes[:].bitcast(FP8X4), lhsT_scale=q_plane[:],
                            rhs=keys[:, 768:896].bitcast(FP8X4), rhs_scale=keys_plane[:, 768:896], start=True, stop=True)
        nc.vector.tensor_copy(out=a[:, 768:896], in_=a_bank3[:])
        a_bank4 = ps.tile([P, 128], F32)
        nc.tensor.matmul_mx(out=a_bank4[:], lhsT=q_codes[:].bitcast(FP8X4), lhsT_scale=q_plane[:],
                            rhs=keys[:, 896:1024].bitcast(FP8X4), rhs_scale=keys_plane[:, 896:1024], start=True, stop=True)
        nc.vector.tensor_copy(out=a[:, 896:1024], in_=a_bank4[:])

        first, second = slice(0, HALF), slice(HALF, I)
        first_cols, second_cols = slice(0, HALF_COLS), slice(HALF_COLS, LIST_COLS)

        r = sb.tile([P, I], F32)
        b_first = sb.tile([P, HALF], F32)
        nc.scalar.activation(out=b_first[:], in_=b[:].indirect(idx2[:, first_cols]), func=COPY)
        diff_first = sb.tile([P, HALF], F32, tag="diff")
        nc.vector.tensor_tensor(
            out=diff_first[:], in0=a[:].indirect(idx[:, first_cols]), in1=b_first[:], op=ALU.subtract
        )
        nc.vector.tensor_scalar_max(out=r[:, first], in0=diff_first[:], scalar1=0.0)
        nc.vector.tensor_copy(out=f1[:].indirect(idx[:, first_cols]), in_=r[:, first])

        b_second = sb.tile([P, HALF], F32)
        nc.scalar.activation(out=b_second[:], in_=b[:].indirect(idx2[:, second_cols]), func=COPY)
        a_second = sb.tile([P, HALF], F32, tag="a_second_then_f2")
        nc.scalar.activation(out=a_second[:], in_=a[:].indirect(idx[:, second_cols]), func=COPY)
        diff_second = sb.tile([P, HALF], F32, tag="diff")
        nc.gpsimd.tensor_tensor(out=diff_second[:], in0=a_second[:], in1=b_second[:], op=ALU.subtract)
        nc.scalar.activation(out=r[:, second], in_=diff_second[:], func=RELU)
        f2 = sb.tile([P, U], F32, tag="a_second_then_f2")
        nc.gpsimd.memset(f2[:], 0.0)
        nc.vector.tensor_copy(out=f1[:].indirect(idx[:, second_cols]), in_=r[:, second])

        nc.vector.tensor_copy(out=f2[:].indirect(idx2[:]), in_=r[:])

        aa = sb.tile([P, T], F32)
        nc.gpsimd.tensor_tensor(out=aa[:], in0=a[:], in1=f1[:], op=ALU.subtract)
        aa_first = sb.tile([P, HALF], F32)
        nc.scalar.activation(out=aa_first[:], in_=aa[:].indirect(idx3[:, first_cols]), func=COPY)
        aa_second = sb.tile([P, HALF], F32)
        nc.scalar.activation(out=aa_second[:], in_=aa[:].indirect(idx3[:, second_cols]), func=COPY)

        bb = sb.tile([P, U], F32)
        nc.vector.tensor_tensor(out=bb[:], in0=b[:], in1=f2[:], op=ALU.add)
        bb_first = sb.tile([P, HALF], F32)
        nc.vector.tensor_copy(out=bb_first[:], in_=bb[:].indirect(idx4[:, first_cols]))
        bb_second = sb.tile([P, HALF], F32)
        nc.scalar.activation(out=bb_second[:], in_=bb[:].indirect(idx4[:, second_cols]), func=COPY)
        y0 = sb.tile([P, 256], F32)
        nc.vector.tensor_tensor(out=y0[:], in0=aa_first[:, 0:256], in1=bb_first[:, 0:256], op=ALU.min)
        nc.sync.dma_start(out=out[:, 0:256], in_=y0[:])
        y1 = sb.tile([P, 256], F32)
        nc.vector.tensor_tensor(out=y1[:], in0=aa_second[:, 0:256], in1=bb_second[:, 0:256], op=ALU.min)
        nc.sync.dma_start(out=out[:, 256:512], in_=y1[:])
